import numpy as np
import ml_dtypes


def mxq(x, axis, fmt="e4m3"):
    dtype, down = {"e4m3": (ml_dtypes.float8_e4m3fn, 7), "e5m2": (ml_dtypes.float8_e5m2, 14)}[fmt]
    v = np.moveaxis(np.asarray(x, np.float32).astype(ml_dtypes.bfloat16).astype(np.float64), axis, -1)
    blocks = v.reshape(v.shape[:-1] + (-1, 32))
    amax = np.abs(blocks).max(-1, keepdims=True)
    byte = np.maximum(np.where(amax > 0, np.frexp(amax)[1] - 1 + 127, 0) - down, 1)
    scale = np.exp2(byte - 127.0)
    codes = (blocks / scale).astype(np.float32).astype(dtype).astype(np.float64)
    return np.moveaxis((codes * scale).reshape(v.shape), -1, axis)


WIDE = False


def mx_kscale(k):
    if not WIDE:
        return np.ones(k)
    levels = np.array([30, -30])
    if k % 512:
        return np.exp2(np.random.permutation(np.resize(levels, k // 32))).repeat(32)
    a = np.empty((k // 512, 16))
    for p in range(k // 512):
        a[p, :8] = np.random.permutation(np.resize(levels, 8))
        for g in range(8):
            far = levels[np.abs(levels - a[p, g]) >= 10]
            a[p, g + 8] = far[np.random.randint(len(far))]
    return np.exp2(a.ravel()).repeat(32)


def f64(x):
    return np.asarray(x).astype(np.float64)


def striped(idx):
    return np.tile(np.asarray(idx).reshape(-1, 16).T, (8, 1)).astype(np.uint16)


def unstriped(offs):
    return offs[:16].T.reshape(-1).astype(np.int64)


E2M1 = np.array([0.0, 0.5, 1.0, 1.5, 2.0, 3.0, 4.0, 6.0, -0.0, -0.5, -1.0, -1.5, -2.0, -3.0, -4.0, -6.0])


def pack_weight(w, fmt):
    k, n = w.shape
    w = f64(np.asarray(w, np.float32).astype(ml_dtypes.bfloat16)).reshape(k // 32, 32, n)
    amax = np.abs(w).max(1)
    if fmt in ("e4m3", "e5m2"):
        byte = np.frexp(amax)[1] - 1 + 127 - (7 if fmt == "e4m3" else 14)
    else:
        mant, ex = np.frexp(amax / 6.0)
        byte = np.where(mant > 0.5, ex, ex - 1) + 127
    byte = np.clip(np.where(amax > 0, byte, 1), 1, 254)
    scaled = (w * np.exp2(127.0 - byte)[:, None, :]).reshape(k, n).astype(np.float32)
    by_word = np.ascontiguousarray(scaled.reshape(k // 512, 128, 4, n).transpose(0, 1, 3, 2))
    if fmt in ("e4m3", "e5m2"):
        words = by_word.astype(ml_dtypes.float8_e4m3fn if fmt == "e4m3" else ml_dtypes.float8_e5m2).view(np.uint8)
    else:
        c = by_word.astype(ml_dtypes.float4_e2m1fn).view(np.uint8) & 0xF
        words = (c[..., 0::2] | (c[..., 1::2] << 4)).reshape(k // 512, 128, 2 * n)
    return np.ascontiguousarray(words), np.ascontiguousarray(byte.astype(np.uint8).reshape(k // 512, 16, n))


def unpack_weight(words, scales, fmt):
    g, _, n = scales.shape
    words = np.ascontiguousarray(words).reshape(g, 128, n, -1)
    if fmt in ("e4m3", "e5m2"):
        vals = words.view(ml_dtypes.float8_e4m3fn if fmt == "e4m3" else ml_dtypes.float8_e5m2).astype(np.float64)
    else:
        nib = np.empty((g, 128, n, 4), np.uint8)
        nib[..., 0::2] = words & 0xF
        nib[..., 1::2] = words >> 4
        vals = E2M1[nib]
    vals = vals * np.repeat(np.exp2(scales.astype(np.float64) - 127.0), 8, axis=1)[..., None]
    return vals.transpose(0, 1, 3, 2).reshape(g * 512, n)


def sigmoid(v):
    return 1.0 / (1.0 + np.exp(-v))


K, F, T, Z, J, R, O, N, E = 512, 512, 1024, 1024, 256, 512, 128, 256, 512


def setup_inputs():
    n = np.random.standard_normal
    idx = np.random.permutation(T)[:J]
    idx2 = np.random.permutation(Z)[:J]
    idx3 = np.random.permutation(J)[:O]
    idx4 = np.random.permutation(J)[:O]
    idx5 = np.random.permutation(E)[:O]
    fk = mx_kscale(K)
    ff = mx_kscale(F)
    fr = mx_kscale(R)
    xtp = pack_weight(n((K, T)) / fk[:, None], "e5m2")
    wp = pack_weight(n((K, R)) * 1 / np.sqrt(K) * fk[:, None], "e2m1")
    xop = pack_weight(n((F, Z)) / ff[:, None], "e4m3")
    w2p = pack_weight(n((F, R)) * 1 / np.sqrt(F) * ff[:, None] * fr, "e2m1")
    wbp = pack_weight(n((R, N)) * 1 / np.sqrt(R) / fr[:, None], "e2m1")
    return {
        "xt_words": xtp[0],
        "xt_scales": xtp[1],
        "w_words": wp[0],
        "w_scales": wp[1],
        "xo_words": xop[0],
        "xo_scales": xop[1],
        "w2_words": w2p[0],
        "w2_scales": w2p[1],
        "sg": (np.random.uniform(0.6, 1.6, (R, 1))).astype(np.float32),
        "bg": (np.random.uniform(-1.0, 1.0, (R, 1))).astype(np.float32),
        "wb_words": wbp[0],
        "wb_scales": wbp[1],
        "tz": (n((N, E))).astype(np.float32),
        "so": (np.random.uniform(0.6, 1.6, (N, 1))).astype(np.float32),
        "bo": (np.random.uniform(-1.0, 1.0, (N, 1))).astype(np.float32),
        "offs": striped(idx),
        "offs2": striped(idx2),
        "offs3": striped(idx3),
        "offs4": striped(idx4),
        "offs5": striped(idx5),
    }


def reference(xt_words, xt_scales, w_words, w_scales, xo_words, xo_scales, w2_words, w2_scales, sg, bg, wb_words, wb_scales, tz, so, bo, offs, offs2, offs3, offs4, offs5):
    idx = unstriped(offs)
    idx2 = unstriped(offs2)
    idx3 = unstriped(offs3)
    idx4 = unstriped(offs4)
    idx5 = unstriped(offs5)
    xtu = unpack_weight(xt_words, xt_scales, "e5m2")
    wu = unpack_weight(w_words, w_scales, "e2m1")
    xou = unpack_weight(xo_words, xo_scales, "e4m3")
    w2u = unpack_weight(w2_words, w2_scales, "e2m1")
    wbu = unpack_weight(wb_words, wb_scales, "e2m1")
    xtidxg = xtu[:, idx]
    a = wu.T @ xtidxg
    xoidx2g = xou[:, idx2]
    b = w2u.T @ xoidx2g
    hid = b[:, idx4] * sigmoid(a[:, idx3] * f64(sg) + f64(bg))
    hidq = mxq(hid, 0, "e4m3")
    p = wbu.T @ hidq
    y = p * sigmoid(f64(tz)[:, idx5] * f64(so) + f64(bo))
    return y

@@ -1,0 +1,193 @@
+from contextlib import ExitStack
+
+import concourse.mybir as mybir
+
+F32 = mybir.dt.float32
+BF16 = mybir.dt.bfloat16
+I32 = mybir.dt.int32
+U32 = mybir.dt.uint32
+U16 = mybir.dt.uint16
+U8 = mybir.dt.uint8
+E4M3 = mybir.dt.float8_e4m3fn_x4
+E5M2 = mybir.dt.float8_e5m2_x4
+E2M1 = mybir.dt.float4_e2m1fn_x4
+ACT = mybir.ActivationFunctionType
+MULT = mybir.AluOpType.mult
+
+P = 128
+PACK = 4
+T, J, R, O, N, E = 1024, 256, 512, 128, 256, 512
+FLOPS = 2 * 512 * R * J * 2 + 2 * R * N * O
+
+
+def load_scale_rows(queue, plane, scales, quadrants=range(4)):
+    for q in quadrants:
+        queue.dma_start(out=plane[32 * q : 32 * q + 4, :].bitcast(I32), in_=scales[0, 4 * q : 4 * q + 4, :].bitcast(I32))
+
+
+def tile_list_twotab_gatefetch_one_finalgate_kernel(
+    tc, xt_words, xt_scales, w_words, w_scales, xo_words, xo_scales, w2_words, w2_scales,
+    sg, bg, wb_words, wb_scales, tz, so, bo, offs, offs2, offs3, offs4, offs5, out,
+):
+    nc = tc.nc
+    with ExitStack() as ctx:
+        sb = ctx.enter_context(tc.tile_pool(name="sb", bufs=1))
+        ps = ctx.enter_context(tc.psum_pool(name="ps", bufs=1))
+
+        def tile(shape, dtype, name):
+            return sb.tile(shape, dtype, name=name, align_bytes=64)
+
+        def load_list(src, name):
+            t = sb.tile(list(src.shape), U16, name=name)
+            nc.sync.dma_start(t[:], src)
+            return t
+
+        again = ctx.enter_context(tc.tile_pool(name="again", bufs=1))
+
+        def on_xt(shape, dtype, name, offset):
+            return again.tile(shape, dtype, name=name, align_bytes=64, offset=offset)
+
+        xt_plane = tile([P, T], U8, "xt_plane")
+        xo_plane = tile([P, T], U8, "xo_plane")
+        planes = tile([P, 2 * R + N], U8, "planes")
+        w_plane, w2_plane, wb_plane = planes[:, 0:R], planes[:, R : 2 * R], planes[:, 2 * R : 2 * R + N]
+        nc.vector.memset(xt_plane[:].bitcast(I32), 0)
+        nc.vector.memset(planes[:].bitcast(I32), 0)
+        nc.vector.memset(xo_plane[:].bitcast(I32), 0)
+
+        warm = tile([P, 2], F32, "warm")
+        nc.vector.memset(warm[:, 0:1], 0.0)
+        nc.scalar.activation(out=warm[:, 1:2], in_=warm[:, 0:1], func=ACT.Sigmoid)
+
+        xt_tab = on_xt([P, T], I32, "xt_tab", 0)
+        xo_tab = tile([P, T], I32, "xo_tab")
+        w_raw = tile([P, R // 2], I32, "w_raw")
+        w2_raw = tile([P, R // 2], I32, "w2_raw")
+        wb_raw = tile([P, N // 2], I32, "wb_raw")
+        sg_t = tile([P, PACK], F32, "sg_t")
+        bg_t = tile([P, PACK], F32, "bg_t")
+        so_t = tile([P, 2], F32, "so_t")
+        bo_t = tile([P, 2], F32, "bo_t")
+        tz_t = [tile([P, E], F32, "tz%d" % u) for u in range(2)]
+
+        l1 = load_list(offs, "l1")
+        nc.sync.dma_start(out=w_raw[:], in_=w_words[0].bitcast(I32))
+        load_scale_rows(nc.sync, xt_plane, xt_scales)
+        load_scale_rows(nc.sync, w_plane, w_scales, range(1))
+        nc.scalar.dma_start(out=xt_tab[:], in_=xt_words[0].rearrange("p n t -> p (n t)").bitcast(I32))
+        nc.gpsimd.dma_start(out=xo_tab[:], in_=xo_words[0].rearrange("p n t -> p (n t)").bitcast(I32))
+        nc.gpsimd.dma_start(out=sg_t[:], in_=sg.rearrange("(p t) o -> p (t o)", t=PACK))
+        nc.gpsimd.dma_start(out=bg_t[:], in_=bg.rearrange("(p t) o -> p (t o)", t=PACK))
+        load_scale_rows(nc.sync, w_plane, w_scales, range(1, 4))
+        nc.sync.dma_start(out=w2_raw[:], in_=w2_words[0].bitcast(I32))
+        l2 = load_list(offs2, "l2")
+        load_scale_rows(nc.sync, xo_plane, xo_scales)
+        l3 = load_list(offs3, "l3")
+        load_scale_rows(nc.sync, w2_plane, w2_scales)
+        l4 = load_list(offs4, "l4")
+        for u in range(2):
+            nc.sync.dma_start(out=tz_t[u][:], in_=tz[P * u : P * (u + 1), :])
+        l5 = load_list(offs5, "l5")
+        nc.sync.dma_start(out=wb_raw[:], in_=wb_words[0].bitcast(I32))
+        load_scale_rows(nc.sync, wb_plane, wb_scales)
+        with nc.allow_non_contiguous_dma(reason="one value a partition for each half of the output rows"):
+            nc.gpsimd.dma_start(out=so_t[:], in_=so.rearrange("(u p) o -> p (u o)", p=P))
+            nc.gpsimd.dma_start(out=bo_t[:], in_=bo.rearrange("(u p) o -> p (u o)", p=P))
+
+        def deal(copy, dst, src):
+            copy(
+                out=dst.rearrange("p (t q) -> p t q", t=PACK),
+                in_=src.rearrange("p (q t) -> p t q", t=PACK),
+            )
+
+        def products(w_d, s_d, g_w, g_sc, fmt, name):
+            banks = []
+            for t in range(PACK):
+                acc = ps.tile([P, J], F32, name="%s_acc%d" % (name, t), tag="%s%d" % (name, t))
+                nc.tensor.matmul_mx(
+                    out=acc[:],
+                    lhsT=w_d[:, P * t : P * (t + 1)].bitcast(E2M1),
+                    lhsT_scale=s_d[:, P * t : P * (t + 1)],
+                    rhs=g_w[:].bitcast(fmt),
+                    rhs_scale=g_sc[:],
+                    start=True,
+                    stop=True,
+                )
+                banks.append(acc)
+            return banks
+
+        a_wd = tile([P, R], U16, "a_wd")
+        deal(nc.scalar.copy, a_wd[:], w_raw[:].bitcast(U16))
+        a_gsc = tile([P, J], U8, "a_gsc")
+        nc.vector.tensor_copy(a_gsc[:], xt_plane[:].indirect(l1[:]))
+        a_gw = tile([P, J], U32, "a_gw")
+        nc.vector.tensor_copy(a_gw[:], xt_tab[:].bitcast(U32).indirect(l1[:]))
+        a_sd = on_xt([P, R], U8, "a_sd", 0)
+        deal(nc.vector.tensor_copy, a_sd[:], w_plane)
+        a_banks = products(a_wd, a_sd, a_gw, a_gsc, E5M2, "a")
+
+        b_gw = on_xt([P, J], U32, "b_gw", 512)
+        nc.vector.tensor_copy(b_gw[:], xo_tab[:].bitcast(U32).indirect(l2[:]))
+
+        gate = tile([P, PACK, O], F32, "gate")
+        for t in range(PACK):
+            a_sb = tile([P, J], F32, "a_sb%d" % t)
+            nc.scalar.copy(out=a_sb[:], in_=a_banks[t][:])
+            nc.scalar.activation(
+                out=gate[:, t, :], in_=a_sb[:].indirect(l3[:]), func=ACT.Sigmoid,
+                bias=bg_t[:, t : t + 1], scale=sg_t[:, t : t + 1],
+            )
+
+        b_gsc = on_xt([P, J], U8, "b_gsc", 1536)
+        nc.vector.tensor_copy(b_gsc[:], xo_plane[:].indirect(l2[:]))
+        b_wd = tile([P, R], U16, "b_wd")
+        deal(nc.scalar.copy, b_wd[:], w2_raw[:].bitcast(U16))
+        b_sd = on_xt([P, R], U8, "b_sd", 3072)
+        deal(nc.vector.tensor_copy, b_sd[:], w2_plane)
+        b_banks = products(b_wd, b_sd, b_gw, b_gsc, E4M3, "b")
+
+        picked = tile([P, PACK, O], F32, "picked")
+        b_sb = [sb.tile([P, J], F32, name="b_sb%d" % t, tag="b_sb%d" % t) for t in range(PACK)]
+        for t in range(PACK):
+            if t < 3:
+                nc.vector.tensor_copy(out=b_sb[t][:], in_=b_banks[t][:])
+            else:
+                nc.scalar.copy(out=b_sb[t][:], in_=b_banks[t][:])
+        for t in range(PACK):
+            if t < 3:
+                nc.vector.tensor_copy(picked[:, t, :], b_sb[t][:].indirect(l4[:]))
+            else:
+                nc.scalar.activation(out=picked[:, t, :], in_=b_sb[t][:].indirect(l4[:]), func=ACT.Copy)
+
+        hid = tile([P, O * PACK], BF16, "hid")
+        nc.vector.tensor_tensor(
+            out=hid[:].rearrange("p (c i t) -> p c t i", i=4, t=PACK),
+            in0=picked[:].rearrange("p t (c i) -> p c t i", i=4),
+            in1=gate[:].rearrange("p t (c i) -> p c t i", i=4),
+            op=MULT,
+        )
+        hid_w = tile([P, O], U32, "hid_w")
+        hid_s = tile([P, O], U8, "hid_s")
+        nc.vector.quantize_mx(out=hid_w[:].bitcast(E4M3), scales=hid_s[:], in_=hid[:])
+
+        last = sb.tile([P, 2, O], F32, name="last", tag="b_sb3")
+        for u in range(2):
+            nc.scalar.activation(
+                out=last[:, u, :], in_=tz_t[u][:].indirect(l5[:]), func=ACT.Sigmoid,
+                bias=bo_t[:, u : u + 1], scale=so_t[:, u : u + 1],
+            )
+        prod = ps.tile([P, J], F32, name="prod", tag="a0")
+        wb_codes = wb_raw[:].bitcast(U16)
+        for u in range(2):
+            nc.tensor.matmul_mx(
+                out=prod[:, O * u : O * (u + 1)],
+                lhsT=wb_codes[:, P * u : P * (u + 1)].bitcast(E2M1),
+                lhsT_scale=planes[:, 2 * R + P * u : 2 * R + P * (u + 1)],
+                rhs=hid_w[:].bitcast(E4M3),
+                rhs_scale=hid_s[:],
+                start=True,
+                stop=True,
+            )
+        y = tile([P, 2, O], F32, "y")
+        nc.vector.tensor_tensor(out=y[:].rearrange("p u o -> p (u o)"), in0=prod[:], in1=last[:].rearrange("p u o -> p (u o)"), op=MULT)
+        nc.sync.dma_start(out=out.rearrange("(u p) o -> p u o", p=P), in_=y[:])

@@ -16,13 +16,51 @@ MULT = mybir.AluOpType.mult
 
 P = 128
 PACK = 4
-T, J, R, O, N, E = 1024, 256, 512, 128, 256, 512
-FLOPS = 2 * 512 * R * J * 2 + 2 * R * N * O
+QUADRANTS = 4
+K = 512
+T = 1024
+J, R, O, N, E = 256, 512, 128, 256, 512
+HALVES = N // P
+RUN = 4
+FLOPS = 2 * (2 * K * R * J) + 2 * R * N * O
+
+B_COPIES_ON_SCALAR = (1, 3)
+B_GATHERS_ON_SCALAR = (3,)
+B_GATHER_ORDER = (0, 2, 1, 3)
 
 
-def load_scale_rows(queue, plane, scales, quadrants=range(4)):
-    for q in quadrants:
-        queue.dma_start(out=plane[32 * q : 32 * q + 4, :].bitcast(I32), in_=scales[0, 4 * q : 4 * q + 4, :].bitcast(I32))
+def load_plane(nc, plane, scales):
+    for q in range(QUADRANTS):
+        nc.sync.dma_start(out=plane[32 * q : 32 * q + 4, :].bitcast(I32), in_=scales[0, 4 * q : 4 * q + 4, :].bitcast(I32))
+
+
+def deal_words(nc, dst, src):
+    nc.scalar.copy(out=dst.rearrange("p (t q) -> p t q", t=PACK), in_=src.rearrange("p (q t) -> p t q", t=PACK))
+
+
+def deal_scales(nc, dst, src):
+    for t in range(0, PACK, 2):
+        nc.vector.tensor_copy(
+            out=dst.rearrange("p (t q) -> p t q", t=PACK)[:, t : t + 2, :],
+            in_=src.rearrange("p (q t) -> p t q", t=PACK)[:, t : t + 2, :],
+        )
+
+
+def first_products(nc, psum, name, words, scales, listed_words, listed_scales, fmt):
+    banks = []
+    for t in range(PACK):
+        bank = psum.tile([P, J], F32, name="%s_bank%d" % (name, t), tag="%s%d" % (name, t))
+        nc.tensor.matmul_mx(
+            out=bank[:],
+            lhsT=words[:, P * t : P * (t + 1)].bitcast(E2M1),
+            lhsT_scale=scales[:, P * t : P * (t + 1)],
+            rhs=listed_words[:].bitcast(fmt),
+            rhs_scale=listed_scales[:],
+            start=True,
+            stop=True,
+        )
+        banks.append(bank)
+    return banks
 
 
 def tile_list_twotab_gatefetch_one_finalgate_kernel(
@@ -31,163 +69,138 @@ def tile_list_twotab_gatefetch_one_finalgate_kernel(
 ):
     nc = tc.nc
     with ExitStack() as ctx:
-        sb = ctx.enter_context(tc.tile_pool(name="sb", bufs=1))
-        ps = ctx.enter_context(tc.psum_pool(name="ps", bufs=1))
+        sbuf = ctx.enter_context(tc.tile_pool(name="sbuf", bufs=1))
+        psum = ctx.enter_context(tc.psum_pool(name="psum", bufs=1))
+        shared = ctx.enter_context(tc.tile_pool(name="shared", bufs=1))
 
         def tile(shape, dtype, name):
-            return sb.tile(shape, dtype, name=name, align_bytes=64)
+            return sbuf.tile(shape, dtype, name=name, align_bytes=64)
+
+        def on_xt_bytes(shape, dtype, name, offset):
+            return shared.tile(shape, dtype, name=name, align_bytes=64, offset=offset)
 
         def load_list(src, name):
-            t = sb.tile(list(src.shape), U16, name=name)
-            nc.sync.dma_start(t[:], src)
-            return t
-
-        again = ctx.enter_context(tc.tile_pool(name="again", bufs=1))
-
-        def on_xt(shape, dtype, name, offset):
-            return again.tile(shape, dtype, name=name, align_bytes=64, offset=offset)
+            offsets = sbuf.tile(list(src.shape), U16, name=name)
+            nc.sync.dma_start(offsets[:], src)
+            return offsets
 
         xt_plane = tile([P, T], U8, "xt_plane")
         xo_plane = tile([P, T], U8, "xo_plane")
-        planes = tile([P, 2 * R + N], U8, "planes")
-        w_plane, w2_plane, wb_plane = planes[:, 0:R], planes[:, R : 2 * R], planes[:, 2 * R : 2 * R + N]
+        weight_planes = tile([P, 2 * R + N], U8, "weight_planes")
+        w_plane, w2_plane, wb_plane = weight_planes[:, 0:R], weight_planes[:, R : 2 * R], weight_planes[:, 2 * R :]
         nc.vector.memset(xt_plane[:].bitcast(I32), 0)
-        nc.vector.memset(planes[:].bitcast(I32), 0)
+        nc.vector.memset(weight_planes[:].bitcast(I32), 0)
         nc.vector.memset(xo_plane[:].bitcast(I32), 0)
 
         warm = tile([P, 2], F32, "warm")
         nc.vector.memset(warm[:, 0:1], 0.0)
         nc.scalar.activation(out=warm[:, 1:2], in_=warm[:, 0:1], func=ACT.Sigmoid)
 
-        xt_tab = on_xt([P, T], I32, "xt_tab", 0)
-        xo_tab = tile([P, T], I32, "xo_tab")
-        w_raw = tile([P, R // 2], I32, "w_raw")
-        w2_raw = tile([P, R // 2], I32, "w2_raw")
-        wb_raw = tile([P, N // 2], I32, "wb_raw")
-        sg_t = tile([P, PACK], F32, "sg_t")
-        bg_t = tile([P, PACK], F32, "bg_t")
-        so_t = tile([P, 2], F32, "so_t")
-        bo_t = tile([P, 2], F32, "bo_t")
-        tz_t = [tile([P, E], F32, "tz%d" % u) for u in range(2)]
+        xt_table = on_xt_bytes([P, T], I32, "xt_table", 0)
+        xo_table = tile([P, T], I32, "xo_table")
+        w_loaded = tile([P, R // 2], I32, "w_loaded")
+        w2_loaded = tile([P, R // 2], I32, "w2_loaded")
+        wb_loaded = tile([P, N // 2], I32, "wb_loaded")
+        sg_cols = tile([P, PACK], F32, "sg_cols")
+        bg_cols = tile([P, PACK], F32, "bg_cols")
+        so_cols = tile([P, HALVES], F32, "so_cols")
+        bo_cols = tile([P, HALVES], F32, "bo_cols")
+        tz_rows = [tile([P, E], F32, "tz_rows%d" % u) for u in range(HALVES)]
 
-        l1 = load_list(offs, "l1")
-        nc.sync.dma_start(out=w_raw[:], in_=w_words[0].bitcast(I32))
-        load_scale_rows(nc.sync, xt_plane, xt_scales)
-        load_scale_rows(nc.sync, w_plane, w_scales, range(1))
-        nc.scalar.dma_start(out=xt_tab[:], in_=xt_words[0].rearrange("p n t -> p (n t)").bitcast(I32))
-        nc.gpsimd.dma_start(out=xo_tab[:], in_=xo_words[0].rearrange("p n t -> p (n t)").bitcast(I32))
-        nc.gpsimd.dma_start(out=sg_t[:], in_=sg.rearrange("(p t) o -> p (t o)", t=PACK))
-        nc.gpsimd.dma_start(out=bg_t[:], in_=bg.rearrange("(p t) o -> p (t o)", t=PACK))
-        load_scale_rows(nc.sync, w_plane, w_scales, range(1, 4))
-        nc.sync.dma_start(out=w2_raw[:], in_=w2_words[0].bitcast(I32))
-        l2 = load_list(offs2, "l2")
-        load_scale_rows(nc.sync, xo_plane, xo_scales)
-        l3 = load_list(offs3, "l3")
-        load_scale_rows(nc.sync, w2_plane, w2_scales)
-        l4 = load_list(offs4, "l4")
-        for u in range(2):
-            nc.sync.dma_start(out=tz_t[u][:], in_=tz[P * u : P * (u + 1), :])
-        l5 = load_list(offs5, "l5")
-        nc.sync.dma_start(out=wb_raw[:], in_=wb_words[0].bitcast(I32))
-        load_scale_rows(nc.sync, wb_plane, wb_scales)
+        idx = load_list(offs, "idx")
+        nc.sync.dma_start(out=w_loaded[:], in_=w_words[0].bitcast(I32))
+        load_plane(nc, xt_plane, xt_scales)
+        nc.sync.dma_start(out=w2_loaded[:], in_=w2_words[0].bitcast(I32))
+        nc.scalar.dma_start(out=xt_table[:], in_=xt_words[0].rearrange("p n t -> p (n t)").bitcast(I32))
+        nc.gpsimd.dma_start(out=xo_table[:], in_=xo_words[0].rearrange("p n t -> p (n t)").bitcast(I32))
+        nc.gpsimd.dma_start(out=sg_cols[:], in_=sg.rearrange("(p t) o -> p (t o)", t=PACK))
+        load_plane(nc, w_plane, w_scales)
+        idx2 = load_list(offs2, "idx2")
+        idx3 = load_list(offs3, "idx3")
+        nc.sync.dma_start(out=bg_cols[:], in_=bg.rearrange("(p t) o -> p (t o)", t=PACK))
+        load_plane(nc, xo_plane, xo_scales)
+        load_plane(nc, w2_plane, w2_scales)
+        idx4 = load_list(offs4, "idx4")
+        idx5 = load_list(offs5, "idx5")
         with nc.allow_non_contiguous_dma(reason="one value a partition for each half of the output rows"):
-            nc.gpsimd.dma_start(out=so_t[:], in_=so.rearrange("(u p) o -> p (u o)", p=P))
-            nc.gpsimd.dma_start(out=bo_t[:], in_=bo.rearrange("(u p) o -> p (u o)", p=P))
+            nc.gpsimd.dma_start(out=so_cols[:], in_=so.rearrange("(u p) o -> p (u o)", p=P))
+            nc.gpsimd.dma_start(out=bo_cols[:], in_=bo.rearrange("(u p) o -> p (u o)", p=P))
+        for u in range(HALVES):
+            nc.sync.dma_start(out=tz_rows[u][:], in_=tz[P * u : P * (u + 1), :])
+        nc.sync.dma_start(out=wb_loaded[:], in_=wb_words[0].bitcast(I32))
+        load_plane(nc, wb_plane, wb_scales)
 
-        def deal(copy, dst, src):
-            copy(
-                out=dst.rearrange("p (t q) -> p t q", t=PACK),
-                in_=src.rearrange("p (q t) -> p t q", t=PACK),
-            )
+        w_dealt = tile([P, R], U16, "w_dealt")
+        deal_words(nc, w_dealt[:], w_loaded[:].bitcast(U16))
+        xt_listed_scales = tile([P, J], U8, "xt_listed_scales")
+        nc.vector.tensor_copy(xt_listed_scales[:], xt_plane[:].indirect(idx[:]))
+        xt_listed = tile([P, J], U32, "xt_listed")
+        nc.vector.tensor_copy(xt_listed[:], xt_table[:].bitcast(U32).indirect(idx[:]))
+        w_dealt_scales = on_xt_bytes([P, R], U8, "w_dealt_scales", 0)
+        deal_scales(nc, w_dealt_scales[:], w_plane)
+        a_banks = first_products(nc, psum, "a", w_dealt, w_dealt_scales, xt_listed, xt_listed_scales, E5M2)
 
-        def products(w_d, s_d, g_w, g_sc, fmt, name):
-            banks = []
-            for t in range(PACK):
-                acc = ps.tile([P, J], F32, name="%s_acc%d" % (name, t), tag="%s%d" % (name, t))
-                nc.tensor.matmul_mx(
-                    out=acc[:],
-                    lhsT=w_d[:, P * t : P * (t + 1)].bitcast(E2M1),
-                    lhsT_scale=s_d[:, P * t : P * (t + 1)],
-                    rhs=g_w[:].bitcast(fmt),
-                    rhs_scale=g_sc[:],
-                    start=True,
-                    stop=True,
-                )
-                banks.append(acc)
-            return banks
-
-        a_wd = tile([P, R], U16, "a_wd")
-        deal(nc.scalar.copy, a_wd[:], w_raw[:].bitcast(U16))
-        a_gsc = tile([P, J], U8, "a_gsc")
-        nc.vector.tensor_copy(a_gsc[:], xt_plane[:].indirect(l1[:]))
-        a_gw = tile([P, J], U32, "a_gw")
-        nc.vector.tensor_copy(a_gw[:], xt_tab[:].bitcast(U32).indirect(l1[:]))
-        a_sd = on_xt([P, R], U8, "a_sd", 0)
-        deal(nc.vector.tensor_copy, a_sd[:], w_plane)
-        a_banks = products(a_wd, a_sd, a_gw, a_gsc, E5M2, "a")
-
-        b_gw = on_xt([P, J], U32, "b_gw", 512)
-        nc.vector.tensor_copy(b_gw[:], xo_tab[:].bitcast(U32).indirect(l2[:]))
+        xo_listed = on_xt_bytes([P, J], U32, "xo_listed", R)
+        nc.vector.tensor_copy(xo_listed[:], xo_table[:].bitcast(U32).indirect(idx2[:]))
 
         gate = tile([P, PACK, O], F32, "gate")
         for t in range(PACK):
-            a_sb = tile([P, J], F32, "a_sb%d" % t)
-            nc.scalar.copy(out=a_sb[:], in_=a_banks[t][:])
+            a_rows = tile([P, J], F32, "a_rows%d" % t)
+            nc.scalar.copy(out=a_rows[:], in_=a_banks[t][:])
             nc.scalar.activation(
-                out=gate[:, t, :], in_=a_sb[:].indirect(l3[:]), func=ACT.Sigmoid,
-                bias=bg_t[:, t : t + 1], scale=sg_t[:, t : t + 1],
+                out=gate[:, t, :], in_=a_rows[:].indirect(idx3[:]), func=ACT.Sigmoid,
+                bias=bg_cols[:, t : t + 1], scale=sg_cols[:, t : t + 1],
             )
 
-        b_gsc = on_xt([P, J], U8, "b_gsc", 1536)
-        nc.vector.tensor_copy(b_gsc[:], xo_plane[:].indirect(l2[:]))
-        b_wd = tile([P, R], U16, "b_wd")
-        deal(nc.scalar.copy, b_wd[:], w2_raw[:].bitcast(U16))
-        b_sd = on_xt([P, R], U8, "b_sd", 3072)
-        deal(nc.vector.tensor_copy, b_sd[:], w2_plane)
-        b_banks = products(b_wd, b_sd, b_gw, b_gsc, E4M3, "b")
+        xo_listed_scales = on_xt_bytes([P, J], U8, "xo_listed_scales", R + 4 * J)
+        nc.vector.tensor_copy(xo_listed_scales[:], xo_plane[:].indirect(idx2[:]))
+        w2_dealt = tile([P, R], U16, "w2_dealt")
+        deal_words(nc, w2_dealt[:], w2_loaded[:].bitcast(U16))
+        w2_dealt_scales = on_xt_bytes([P, R], U8, "w2_dealt_scales", R + 4 * J + J)
+        deal_scales(nc, w2_dealt_scales[:], w2_plane)
+        b_banks = first_products(nc, psum, "b", w2_dealt, w2_dealt_scales, xo_listed, xo_listed_scales, E4M3)
 
         picked = tile([P, PACK, O], F32, "picked")
-        b_sb = [sb.tile([P, J], F32, name="b_sb%d" % t, tag="b_sb%d" % t) for t in range(PACK)]
+        b_rows = [sbuf.tile([P, J], F32, name="b_rows%d" % t, tag="b_rows%d" % t) for t in range(PACK)]
         for t in range(PACK):
-            if t < 3:
-                nc.vector.tensor_copy(out=b_sb[t][:], in_=b_banks[t][:])
+            copy = nc.scalar.copy if t in B_COPIES_ON_SCALAR else nc.vector.tensor_copy
+            copy(out=b_rows[t][:], in_=b_banks[t][:])
+        for t in B_GATHER_ORDER:
+            if t in B_GATHERS_ON_SCALAR:
+                nc.scalar.activation(out=picked[:, t, :], in_=b_rows[t][:].indirect(idx4[:]), func=ACT.Copy)
             else:
-                nc.scalar.copy(out=b_sb[t][:], in_=b_banks[t][:])
-        for t in range(PACK):
-            if t < 3:
-                nc.vector.tensor_copy(picked[:, t, :], b_sb[t][:].indirect(l4[:]))
-            else:
-                nc.scalar.activation(out=picked[:, t, :], in_=b_sb[t][:].indirect(l4[:]), func=ACT.Copy)
+                nc.vector.tensor_copy(picked[:, t, :], b_rows[t][:].indirect(idx4[:]))
 
         hid = tile([P, O * PACK], BF16, "hid")
         nc.vector.tensor_tensor(
-            out=hid[:].rearrange("p (c i t) -> p c t i", i=4, t=PACK),
-            in0=picked[:].rearrange("p t (c i) -> p c t i", i=4),
-            in1=gate[:].rearrange("p t (c i) -> p c t i", i=4),
+            out=hid[:].rearrange("p (c i t) -> p c t i", i=RUN, t=PACK),
+            in0=picked[:].rearrange("p t (c i) -> p c t i", i=RUN),
+            in1=gate[:].rearrange("p t (c i) -> p c t i", i=RUN),
             op=MULT,
         )
-        hid_w = tile([P, O], U32, "hid_w")
-        hid_s = tile([P, O], U8, "hid_s")
-        nc.vector.quantize_mx(out=hid_w[:].bitcast(E4M3), scales=hid_s[:], in_=hid[:])
+        hid_words = tile([P, O], U32, "hid_words")
+        hid_plane = tile([P, O], U8, "hid_plane")
+        nc.vector.quantize_mx(out=hid_words[:].bitcast(E4M3), scales=hid_plane[:], in_=hid[:])
 
-        last = sb.tile([P, 2, O], F32, name="last", tag="b_sb3")
-        for u in range(2):
+        last_gate = sbuf.tile([P, HALVES, O], F32, name="last_gate", tag="b_rows%d" % B_GATHERS_ON_SCALAR[-1])
+        for u in range(HALVES):
             nc.scalar.activation(
-                out=last[:, u, :], in_=tz_t[u][:].indirect(l5[:]), func=ACT.Sigmoid,
-                bias=bo_t[:, u : u + 1], scale=so_t[:, u : u + 1],
+                out=last_gate[:, u, :], in_=tz_rows[u][:].indirect(idx5[:]), func=ACT.Sigmoid,
+                bias=bo_cols[:, u : u + 1], scale=so_cols[:, u : u + 1],
             )
-        prod = ps.tile([P, J], F32, name="prod", tag="a0")
-        wb_codes = wb_raw[:].bitcast(U16)
-        for u in range(2):
+
+        wb_codes = wb_loaded[:].bitcast(U16)
+        for u in range(HALVES):
+            product = psum.tile([P, O], F32, name="product%d" % u, tag="a%d" % u)
             nc.tensor.matmul_mx(
-                out=prod[:, O * u : O * (u + 1)],
+                out=product[:],
                 lhsT=wb_codes[:, P * u : P * (u + 1)].bitcast(E2M1),
-                lhsT_scale=planes[:, 2 * R + P * u : 2 * R + P * (u + 1)],
-                rhs=hid_w[:].bitcast(E4M3),
-                rhs_scale=hid_s[:],
+                lhsT_scale=wb_plane[:, P * u : P * (u + 1)],
+                rhs=hid_words[:].bitcast(E4M3),
+                rhs_scale=hid_plane[:],
                 start=True,
                 stop=True,
             )
-        y = tile([P, 2, O], F32, "y")
-        nc.vector.tensor_tensor(out=y[:].rearrange("p u o -> p (u o)"), in0=prod[:], in1=last[:].rearrange("p u o -> p (u o)"), op=MULT)
-        nc.sync.dma_start(out=out.rearrange("(u p) o -> p u o", p=P), in_=y[:])
+            result = tile([P, O], F32, "result%d" % u)
+            nc.vector.tensor_tensor(out=result[:], in0=product[:], in1=last_gate[:, u, :], op=MULT)
+            (nc.sync, nc.scalar)[u].dma_start(out=out[P * u : P * (u + 1), :], in_=result[:])

@@ -24,9 +24,7 @@ HALVES = N // P
 RUN = 4
 FLOPS = 2 * (2 * K * R * J) + 2 * R * N * O
 
-B_COPIES_ON_SCALAR = (1, 3)
-B_GATHERS_ON_SCALAR = (3,)
-B_GATHER_ORDER = (0, 2, 1, 3)
+LAST = PACK - 1
 
 
 def load_plane(nc, plane, scales):
@@ -163,10 +161,10 @@ def tile_list_twotab_gatefetch_one_finalgate_kernel(
         picked = tile([P, PACK, O], F32, "picked")
         b_rows = [sbuf.tile([P, J], F32, name="b_rows%d" % t, tag="b_rows%d" % t) for t in range(PACK)]
         for t in range(PACK):
-            copy = nc.scalar.copy if t in B_COPIES_ON_SCALAR else nc.vector.tensor_copy
+            copy = nc.scalar.copy if t == LAST else nc.vector.tensor_copy
             copy(out=b_rows[t][:], in_=b_banks[t][:])
-        for t in B_GATHER_ORDER:
-            if t in B_GATHERS_ON_SCALAR:
+        for t in range(PACK):
+            if t == LAST:
                 nc.scalar.activation(out=picked[:, t, :], in_=b_rows[t][:].indirect(idx4[:]), func=ACT.Copy)
             else:
                 nc.vector.tensor_copy(picked[:, t, :], b_rows[t][:].indirect(idx4[:]))
@@ -182,7 +180,7 @@ def tile_list_twotab_gatefetch_one_finalgate_kernel(
         hid_plane = tile([P, O], U8, "hid_plane")
         nc.vector.quantize_mx(out=hid_words[:].bitcast(E4M3), scales=hid_plane[:], in_=hid[:])
 
-        last_gate = sbuf.tile([P, HALVES, O], F32, name="last_gate", tag="b_rows%d" % B_GATHERS_ON_SCALAR[-1])
+        last_gate = sbuf.tile([P, HALVES, O], F32, name="last_gate", tag="b_rows%d" % LAST)
         for u in range(HALVES):
             nc.scalar.activation(
                 out=last_gate[:, u, :], in_=tz_rows[u][:].indirect(idx5[:]), func=ACT.Sigmoid,

from contextlib import ExitStack

import concourse.mybir as mybir

F32 = mybir.dt.float32
BF16 = mybir.dt.bfloat16
I32 = mybir.dt.int32
U32 = mybir.dt.uint32
U16 = mybir.dt.uint16
U8 = mybir.dt.uint8
E4M3 = mybir.dt.float8_e4m3fn_x4
E5M2 = mybir.dt.float8_e5m2_x4
E2M1 = mybir.dt.float4_e2m1fn_x4
ACT = mybir.ActivationFunctionType
MULT = mybir.AluOpType.mult

P = 128
PACK = 4
QUADRANTS = 4
K = 512
T = 1024
J, R, O, N, E = 256, 512, 128, 256, 512
HALVES = N // P
RUN = 4
FLOPS = 2 * (2 * K * R * J) + 2 * R * N * O

LAST = PACK - 1


def load_plane(nc, plane, scales):
    for q in range(QUADRANTS):
        nc.sync.dma_start(out=plane[32 * q : 32 * q + 4, :].bitcast(I32), in_=scales[0, 4 * q : 4 * q + 4, :].bitcast(I32))


def deal_words(nc, dst, src):
    nc.scalar.copy(out=dst.rearrange("p (t q) -> p t q", t=PACK), in_=src.rearrange("p (q t) -> p t q", t=PACK))


def deal_scales(nc, dst, src):
    for t in range(0, PACK, 2):
        nc.vector.tensor_copy(
            out=dst.rearrange("p (t q) -> p t q", t=PACK)[:, t : t + 2, :],
            in_=src.rearrange("p (q t) -> p t q", t=PACK)[:, t : t + 2, :],
        )


def first_products(nc, psum, name, words, scales, listed_words, listed_scales, fmt):
    banks = []
    for t in range(PACK):
        bank = psum.tile([P, J], F32, name="%s_bank%d" % (name, t), tag="%s%d" % (name, t))
        nc.tensor.matmul_mx(
            out=bank[:],
            lhsT=words[:, P * t : P * (t + 1)].bitcast(E2M1),
            lhsT_scale=scales[:, P * t : P * (t + 1)],
            rhs=listed_words[:].bitcast(fmt),
            rhs_scale=listed_scales[:],
            start=True,
            stop=True,
        )
        banks.append(bank)
    return banks


def tile_list_twotab_gatefetch_one_finalgate_kernel(
    tc, xt_words, xt_scales, w_words, w_scales, xo_words, xo_scales, w2_words, w2_scales,
    sg, bg, wb_words, wb_scales, tz, so, bo, offs, offs2, offs3, offs4, offs5, out,
):
    nc = tc.nc
    with ExitStack() as ctx:
        sbuf = ctx.enter_context(tc.tile_pool(name="sbuf", bufs=1))
        psum = ctx.enter_context(tc.psum_pool(name="psum", bufs=1))
        shared = ctx.enter_context(tc.tile_pool(name="shared", bufs=1))

        def tile(shape, dtype, name):
            return sbuf.tile(shape, dtype, name=name, align_bytes=64)

        def on_xt_bytes(shape, dtype, name, offset):
            return shared.tile(shape, dtype, name=name, align_bytes=64, offset=offset)

        def load_list(src, name):
            offsets = sbuf.tile(list(src.shape), U16, name=name)
            nc.sync.dma_start(offsets[:], src)
            return offsets

        xt_plane = tile([P, T], U8, "xt_plane")
        xo_plane = tile([P, T], U8, "xo_plane")
        weight_planes = tile([P, 2 * R + N], U8, "weight_planes")
        w_plane, w2_plane, wb_plane = weight_planes[:, 0:R], weight_planes[:, R : 2 * R], weight_planes[:, 2 * R :]
        nc.vector.memset(xt_plane[:].bitcast(I32), 0)
        nc.vector.memset(weight_planes[:].bitcast(I32), 0)
        nc.vector.memset(xo_plane[:].bitcast(I32), 0)

        warm = tile([P, 2], F32, "warm")
        nc.vector.memset(warm[:, 0:1], 0.0)
        nc.scalar.activation(out=warm[:, 1:2], in_=warm[:, 0:1], func=ACT.Sigmoid)

        xt_table = on_xt_bytes([P, T], I32, "xt_table", 0)
        xo_table = tile([P, T], I32, "xo_table")
        w_loaded = tile([P, R // 2], I32, "w_loaded")
        w2_loaded = tile([P, R // 2], I32, "w2_loaded")
        wb_loaded = tile([P, N // 2], I32, "wb_loaded")
        sg_cols = tile([P, PACK], F32, "sg_cols")
        bg_cols = tile([P, PACK], F32, "bg_cols")
        so_cols = tile([P, HALVES], F32, "so_cols")
        bo_cols = tile([P, HALVES], F32, "bo_cols")
        tz_rows = [tile([P, E], F32, "tz_rows%d" % u) for u in range(HALVES)]

        idx = load_list(offs, "idx")
        nc.sync.dma_start(out=w_loaded[:], in_=w_words[0].bitcast(I32))
        load_plane(nc, xt_plane, xt_scales)
        nc.sync.dma_start(out=w2_loaded[:], in_=w2_words[0].bitcast(I32))
        nc.scalar.dma_start(out=xt_table[:], in_=xt_words[0].rearrange("p n t -> p (n t)").bitcast(I32))
        nc.gpsimd.dma_start(out=xo_table[:], in_=xo_words[0].rearrange("p n t -> p (n t)").bitcast(I32))
        nc.gpsimd.dma_start(out=sg_cols[:], in_=sg.rearrange("(p t) o -> p (t o)", t=PACK))
        load_plane(nc, w_plane, w_scales)
        idx2 = load_list(offs2, "idx2")
        idx3 = load_list(offs3, "idx3")
        nc.sync.dma_start(out=bg_cols[:], in_=bg.rearrange("(p t) o -> p (t o)", t=PACK))
        load_plane(nc, xo_plane, xo_scales)
        load_plane(nc, w2_plane, w2_scales)
        idx4 = load_list(offs4, "idx4")
        idx5 = load_list(offs5, "idx5")
        with nc.allow_non_contiguous_dma(reason="one value a partition for each half of the output rows"):
            nc.gpsimd.dma_start(out=so_cols[:], in_=so.rearrange("(u p) o -> p (u o)", p=P))
            nc.gpsimd.dma_start(out=bo_cols[:], in_=bo.rearrange("(u p) o -> p (u o)", p=P))
        for u in range(HALVES):
            nc.sync.dma_start(out=tz_rows[u][:], in_=tz[P * u : P * (u + 1), :])
        nc.sync.dma_start(out=wb_loaded[:], in_=wb_words[0].bitcast(I32))
        load_plane(nc, wb_plane, wb_scales)

        w_dealt = tile([P, R], U16, "w_dealt")
        deal_words(nc, w_dealt[:], w_loaded[:].bitcast(U16))
        xt_listed_scales = tile([P, J], U8, "xt_listed_scales")
        nc.vector.tensor_copy(xt_listed_scales[:], xt_plane[:].indirect(idx[:]))
        xt_listed = tile([P, J], U32, "xt_listed")
        nc.vector.tensor_copy(xt_listed[:], xt_table[:].bitcast(U32).indirect(idx[:]))
        w_dealt_scales = on_xt_bytes([P, R], U8, "w_dealt_scales", 0)
        deal_scales(nc, w_dealt_scales[:], w_plane)
        a_banks = first_products(nc, psum, "a", w_dealt, w_dealt_scales, xt_listed, xt_listed_scales, E5M2)

        xo_listed = on_xt_bytes([P, J], U32, "xo_listed", R)
        nc.vector.tensor_copy(xo_listed[:], xo_table[:].bitcast(U32).indirect(idx2[:]))

        gate = tile([P, PACK, O], F32, "gate")
        for t in range(PACK):
            a_rows = tile([P, J], F32, "a_rows%d" % t)
            nc.scalar.copy(out=a_rows[:], in_=a_banks[t][:])
            nc.scalar.activation(
                out=gate[:, t, :], in_=a_rows[:].indirect(idx3[:]), func=ACT.Sigmoid,
                bias=bg_cols[:, t : t + 1], scale=sg_cols[:, t : t + 1],
            )

        xo_listed_scales = on_xt_bytes([P, J], U8, "xo_listed_scales", R + 4 * J)
        nc.vector.tensor_copy(xo_listed_scales[:], xo_plane[:].indirect(idx2[:]))
        w2_dealt = tile([P, R], U16, "w2_dealt")
        deal_words(nc, w2_dealt[:], w2_loaded[:].bitcast(U16))
        w2_dealt_scales = on_xt_bytes([P, R], U8, "w2_dealt_scales", R + 4 * J + J)
        deal_scales(nc, w2_dealt_scales[:], w2_plane)
        b_banks = first_products(nc, psum, "b", w2_dealt, w2_dealt_scales, xo_listed, xo_listed_scales, E4M3)

        picked = tile([P, PACK, O], F32, "picked")
        b_rows = [sbuf.tile([P, J], F32, name="b_rows%d" % t, tag="b_rows%d" % t) for t in range(PACK)]
        for t in range(PACK):
            copy = nc.scalar.copy if t == LAST else nc.vector.tensor_copy
            copy(out=b_rows[t][:], in_=b_banks[t][:])
        for t in range(PACK):
            if t == LAST:
                nc.scalar.activation(out=picked[:, t, :], in_=b_rows[t][:].indirect(idx4[:]), func=ACT.Copy)
            else:
                nc.vector.tensor_copy(picked[:, t, :], b_rows[t][:].indirect(idx4[:]))

        hid = tile([P, O * PACK], BF16, "hid")
        nc.vector.tensor_tensor(
            out=hid[:].rearrange("p (c i t) -> p c t i", i=RUN, t=PACK),
            in0=picked[:].rearrange("p t (c i) -> p c t i", i=RUN),
            in1=gate[:].rearrange("p t (c i) -> p c t i", i=RUN),
            op=MULT,
        )
        hid_words = tile([P, O], U32, "hid_words")
        hid_plane = tile([P, O], U8, "hid_plane")
        nc.vector.quantize_mx(out=hid_words[:].bitcast(E4M3), scales=hid_plane[:], in_=hid[:])

        last_gate = sbuf.tile([P, HALVES, O], F32, name="last_gate", tag="b_rows%d" % LAST)
        for u in range(HALVES):
            nc.scalar.activation(
                out=last_gate[:, u, :], in_=tz_rows[u][:].indirect(idx5[:]), func=ACT.Sigmoid,
                bias=bo_cols[:, u : u + 1], scale=so_cols[:, u : u + 1],
            )

        wb_codes = wb_loaded[:].bitcast(U16)
        for u in range(HALVES):
            product = psum.tile([P, O], F32, name="product%d" % u, tag="a%d" % u)
            nc.tensor.matmul_mx(
                out=product[:],
                lhsT=wb_codes[:, P * u : P * (u + 1)].bitcast(E2M1),
                lhsT_scale=wb_plane[:, P * u : P * (u + 1)],
                rhs=hid_words[:].bitcast(E4M3),
                rhs_scale=hid_plane[:],
                start=True,
                stop=True,
            )
            result = tile([P, O], F32, "result%d" % u)
            nc.vector.tensor_tensor(out=result[:], in0=product[:], in1=last_gate[:, u, :], op=MULT)
            (nc.sync, nc.scalar)[u].dma_start(out=out[P * u : P * (u + 1), :], in_=result[:])
